import numpy as np
import ml_dtypes


def mxq(x, axis, fmt="e4m3"):
    dtype, down = {"e4m3": (ml_dtypes.float8_e4m3fn, 7), "e5m2": (ml_dtypes.float8_e5m2, 14)}[fmt]
    v = np.moveaxis(np.asarray(x, np.float32).astype(ml_dtypes.bfloat16).astype(np.float64), axis, -1)
    blocks = v.reshape(v.shape[:-1] + (-1, 32))
    amax = np.abs(blocks).max(-1, keepdims=True)
    byte = np.maximum(np.where(amax > 0, np.frexp(amax)[1] - 1 + 127, 0) - down, 1)
    scale = np.exp2(byte - 127.0)
    codes = (blocks / scale).astype(np.float32).astype(dtype).astype(np.float64)
    return np.moveaxis((codes * scale).reshape(v.shape), -1, axis)


WIDE = False


def mx_kscale(k):
    if not WIDE:
        return np.ones(k)
    levels = np.array([24, -24, 12, -12, 0])
    if k % 512:
        return np.exp2(np.random.permutation(np.resize(levels, k // 32))).repeat(32)
    a = np.empty((k // 512, 16))
    for p in range(k // 512):
        a[p, :8] = np.random.permutation(np.resize(levels, 8))
        for g in range(8):
            far = levels[np.abs(levels - a[p, g]) >= 10]
            a[p, g + 8] = far[np.random.randint(len(far))]
    return np.exp2(a.ravel()).repeat(32)


def f64(x):
    return np.asarray(x).astype(np.float64)


def striped8(idx):
    return np.concatenate([v.reshape(-1, 16).T for v in idx]).astype(np.uint16)


def unstriped8(offs):
    return np.stack([offs[16 * g:16 * g + 16].T.reshape(-1) for g in range(8)]).astype(np.int64)


E2M1 = np.array([0.0, 0.5, 1.0, 1.5, 2.0, 3.0, 4.0, 6.0, -0.0, -0.5, -1.0, -1.5, -2.0, -3.0, -4.0, -6.0])


def pack_weight(w, fmt):
    k, n = w.shape
    w = f64(np.asarray(w, np.float32).astype(ml_dtypes.bfloat16)).reshape(k // 32, 32, n)
    amax = np.abs(w).max(1)
    if fmt == "e4m3":
        byte = np.frexp(amax)[1] - 1 + 127 - 7
    else:
        mant, ex = np.frexp(amax / 6.0)
        byte = np.where(mant > 0.5, ex, ex - 1) + 127
    byte = np.clip(np.where(amax > 0, byte, 1), 1, 254)
    scaled = (w * np.exp2(127.0 - byte)[:, None, :]).reshape(k, n).astype(np.float32)
    by_word = np.ascontiguousarray(scaled.reshape(k // 512, 128, 4, n).transpose(0, 1, 3, 2))
    if fmt == "e4m3":
        words = by_word.astype(ml_dtypes.float8_e4m3fn).view(np.uint8)
    else:
        c = by_word.astype(ml_dtypes.float4_e2m1fn).view(np.uint8) & 0xF
        words = (c[..., 0::2] | (c[..., 1::2] << 4)).reshape(k // 512, 128, 2 * n)
    return np.ascontiguousarray(words), np.ascontiguousarray(byte.astype(np.uint8).reshape(k // 512, 16, n))


def unpack_weight(words, scales, fmt):
    g, _, n = scales.shape
    words = np.ascontiguousarray(words).reshape(g, 128, n, -1)
    if fmt == "e4m3":
        vals = words.view(ml_dtypes.float8_e4m3fn).astype(np.float64)
    else:
        nib = np.empty((g, 128, n, 4), np.uint8)
        nib[..., 0::2] = words & 0xF
        nib[..., 1::2] = words >> 4
        vals = E2M1[nib]
    vals = vals * np.repeat(np.exp2(scales.astype(np.float64) - 127.0), 8, axis=1)[..., None]
    return vals.transpose(0, 1, 3, 2).reshape(g * 512, n)


def planes(y):
    n, m = y.shape
    v = y.astype(np.float32).astype(ml_dtypes.bfloat16).astype(np.float64).reshape(n // 32, 32, m)
    top = np.abs(v).max(1)
    byte = np.clip(np.where(top > 0, np.frexp(top)[1] - 1 + 127 - 7, 1), 1, 254)
    codes = (v * np.exp2(127.0 - byte)[:, None, :]).reshape(n, m).astype(np.float32).astype(ml_dtypes.float8_e4m3fn).view(np.uint8)
    words = codes.reshape(n // 512, 128, 4, m).transpose(0, 1, 3, 2)
    return np.ascontiguousarray(words), np.ascontiguousarray(byte.astype(np.uint8).reshape(n // 512, 16, m))


def silu(f):
    return f / (1.0 + np.exp(-np.maximum(f, -700.0)))


K, L, N, T, J = 512, 512, 512, 2048, 1024


def setup_inputs():
    n = np.random.standard_normal
    s = mx_kscale(K)[:, None]
    s2 = mx_kscale(L)[:, None]
    p_wa = pack_weight(n((K, N)) / np.sqrt(K) / s, "e2m1")
    return {
        "xT": (n((K, T)) * s).astype(np.float32),
        "wgt": np.repeat(np.random.uniform(0.5, 2.0, (8, J)), 16, axis=0).astype(np.float32),
        "zT": (n((L, T)) * s2).astype(np.float32),
        "wgt2": np.repeat(np.random.uniform(0.5, 2.0, (8, J)), 16, axis=0).astype(np.float32),
        "wa_words": p_wa[0],
        "wa_scales": p_wa[1],
        "wb": (n((L, N)) / np.sqrt(L) / s2).astype(np.float32),
        "res": (n((N, J))).astype(np.float32),
        "offs": striped8(np.stack([np.random.permutation(T)[:J] for _ in range(8)])),
        "offs2": striped8(np.stack([np.random.permutation(T)[:J] for _ in range(8)])),
    }


def reference(xT, wgt, zT, wgt2, wa_words, wa_scales, wb, res, offs, offs2):
    idx = unstriped8(offs)
    idx2 = unstriped8(offs2)
    rows = np.arange(K)
    xg = f64(wgt)[rows // 4 % 128] * f64(xT)[rows[:, None], idx[rows % 512 // 64]]
    xT_ = mxq(xg, 0, "e4m3")
    rows = np.arange(L)
    xg = f64(wgt2)[rows // 4 % 128] * f64(zT)[rows[:, None], idx2[rows % 512 // 64]]
    zT_ = mxq(xg, 0, "e4m3")
    wa_ = unpack_weight(wa_words, wa_scales, "e2m1")
    wb_ = mxq(f64(wb), 0, "e4m3")
    ya = wa_.T @ xT_
    yb = wb_.T @ zT_
    out_0 = silu(ya) * yb + f64(res)
    return (out_0,) + planes(out_0)

@@ -1,0 +1,220 @@
+from contextlib import ExitStack
+
+import concourse.mybir as mybir
+
+K, L, N, T, J = 512, 512, 512, 2048, 1024
+FLOPS = 2 * (K + L) * N * J
+
+F32 = mybir.dt.float32
+BF16 = mybir.dt.bfloat16
+I32 = mybir.dt.int32
+U32 = mybir.dt.uint32
+U16 = mybir.dt.uint16
+U8 = mybir.dt.uint8
+FP8X4 = mybir.dt.float8_e4m3fn_x4
+FP4X4 = mybir.dt.float4_e2m1fn_x4
+MULT = mybir.AluOpType.mult
+ADD = mybir.AluOpType.add
+SILU = mybir.ActivationFunctionType.Silu
+
+P = 128
+PACK = 4
+HALF = 512
+WIDTHS = [128, 256, 256, 256, 128]
+STARTS = [sum(WIDTHS[:c]) for c in range(len(WIDTHS))]
+NCH = len(WIDTHS)
+
+
+def tile_list_glu_resP_kernel(
+    tc, xT, wgt, zT, wgt2, wa_words, wa_scales, wb, res, offs, offs2, out_0, out_1, out_2
+):
+    nc = tc.nc
+    with ExitStack() as ctx:
+        keep = ctx.enter_context(tc.tile_pool(name="keep", bufs=1))
+        psum = ctx.enter_context(tc.psum_pool(name="psum", bufs=1))
+
+        def sb(shape, dtype, name, tag=None):
+            return keep.tile(shape, dtype, name=name, tag=tag or name, align_bytes=64)
+
+        x_offs = keep.tile([P, J // 16], U16, name="x_offs")
+        z_offs = keep.tile([P, J // 16], U16, name="z_offs")
+        x_planes = [sb([P, T], F32, "x_plane%d" % i) for i in range(PACK)]
+        z_planes = [sb([P, T], F32, "z_plane%d" % i) for i in range(PACK)]
+        x_wgt = sb([P, J], F32, "x_wgt")
+        z_wgt = sb([P, J], F32, "z_wgt")
+        wa_raw = sb([P, 2 * N], U8, "wa_raw")
+        wa_sc_raw = sb([P, N], U8, "wa_sc_raw")
+        wa_codes = sb([P, 2 * N], U8, "wa_codes")
+        wa_sc = sb([P, N], U8, "wa_sc")
+        wb_raw = sb([P, PACK, N], F32, "wb_raw")
+        wb_bf = sb([P, N * PACK], BF16, "wb_bf")
+        wb_sc = sb([P, N], U8, "wb_sc")
+        res_t = [sb([P, PACK, WIDTHS[c]], F32, "res%d" % c) for c in range(NCH)]
+        warm = sb([P, 2], F32, "warm")
+
+        cols = [slice(STARTS[c], STARTS[c] + WIDTHS[c]) for c in range(NCH)]
+        x_rows = xT.rearrange("(p i) t -> p i t", i=PACK)
+        z_rows = zT.rearrange("(p i) t -> p i t", i=PACK)
+        res_rows = res.rearrange("(p t) j -> p t j", t=PACK)
+        out_rows = out_0.rearrange("(p t) j -> p t j", t=PACK)
+        out_words = out_1[0].rearrange("p j i -> p (j i)").bitcast(I32)
+        out_scales = out_2[0].bitcast(I32)
+
+        nc.gpsimd.memset(wa_sc_raw[:].bitcast(I32), 0)
+        nc.gpsimd.memset(warm[:, 0:1], 0.0)
+        nc.scalar.activation(warm[:, 1:2], warm[:, 0:1], SILU)
+
+        nc.sync.dma_start(x_offs[:], offs)
+        nc.sync.dma_start(wa_raw[:].bitcast(I32), wa_words[0].bitcast(I32))
+        nc.sync.dma_start(x_wgt[:, 0:HALF], wgt[:, 0:HALF])
+        nc.sync.dma_start(x_planes[0][:], x_rows[:, 0, :])
+        nc.sync.dma_start(x_wgt[:, HALF:J], wgt[:, HALF:J])
+        for q in range(4):
+            nc.sync.dma_start(
+                wa_sc_raw[32 * q : 32 * q + 4, :].bitcast(I32), wa_scales[0, 4 * q : 4 * q + 4, :].bitcast(I32)
+            )
+        for i in range(1, PACK):
+            nc.sync.dma_start(x_planes[i][:], x_rows[:, i, :])
+        nc.sync.dma_start(z_offs[:], offs2)
+        nc.sync.dma_start(z_planes[0][:], z_rows[:, 0, :])
+        nc.sync.dma_start(z_wgt[:], wgt2)
+        nc.sync.dma_start(z_planes[1][:], z_rows[:, 1, :])
+        nc.sync.dma_start(wb_raw[:], wb.rearrange("(p i) n -> p i n", i=PACK))
+        for i in range(2, PACK):
+            nc.sync.dma_start(z_planes[i][:], z_rows[:, i, :])
+        for c in range(NCH):
+            nc.sync.dma_start(res_t[c][:], res_rows[:, :, cols[c]])
+
+        def weave(dst, src):
+            nc.scalar.copy(
+                dst.rearrange("p (c i t) -> p c t i", i=4, t=PACK),
+                src.rearrange("p t (c i) -> p c t i", i=4),
+            )
+
+        nc.vector.tensor_copy(
+            wa_codes[:].rearrange("p (t m b) -> p m t b", t=PACK, b=2),
+            wa_raw[:].rearrange("p (m t b) -> p m t b", t=PACK, b=2),
+        )
+
+        xg = sb([P, PACK, J], F32, "xg")
+        x_bf = [sb([P, HALF * PACK], BF16, "x_bf%d" % h) for h in range(2)]
+        x_sc = [sb([P, HALF], U8, "x_sc%d" % h) for h in range(2)]
+
+        def gather(dst, plane, lists, weights, span):
+            nc.vector.tensor_tensor(
+                dst[:, span], plane[:].indirect(lists[:, span.start // 16 : span.stop // 16]), weights[:, span], MULT
+            )
+
+        halves = [slice(0, HALF), slice(HALF, J)]
+        for span in halves:
+            gather(xg[:, 0, :], x_planes[0], x_offs, x_wgt, span)
+        nc.vector.tensor_copy(
+            wa_sc[:].rearrange("p (t m) -> p m t", t=PACK),
+            wa_sc_raw[:].rearrange("p (m t) -> p m t", t=PACK),
+        )
+        for i in range(1, PACK - 1):
+            gather(xg[:, i, :], x_planes[i], x_offs, x_wgt, slice(0, J))
+        for h in range(2):
+            gather(xg[:, PACK - 1, :], x_planes[PACK - 1], x_offs, x_wgt, halves[h])
+            weave(x_bf[h][:], xg[:, :, halves[h]])
+
+        zg = sb([P, PACK, J], F32, "zg")
+        z_bf = [sb([P, WIDTHS[c] * PACK], BF16, "z_bf%d" % c) for c in range(NCH)]
+        z_codes = sb([P, J], U32, "z_codes")
+        z_sc = sb([P, J], U8, "z_sc")
+        gate = [sb([P, PACK, WIDTHS[c]], F32, "gate%d" % c) for c in range(NCH)]
+        prod = [sb([P, PACK, WIDTHS[c]], F32, "prod%d" % c) for c in range(NCH)]
+        y = [sb([P, PACK, WIDTHS[c]], F32, "y%d" % c) for c in range(NCH)]
+        y_bf = [sb([P, WIDTHS[c] * PACK], BF16, "y_bf%d" % c) for c in range(NCH)]
+        y_codes = sb([P, J], U32, "y_codes")
+        y_sc = sb([P, J], U8, "y_sc")
+
+        def quant(codes, scales, src):
+            nc.vector.quantize_mx(out=codes.bitcast(FP8X4), scales=scales, in_=src)
+
+        def product(c, tags, w_cols, w_sc, pieces):
+            per_bank = PACK // len(tags)
+            banks = [psum.tile([P, per_bank, WIDTHS[c]], F32, name="ps", tag=tag) for tag in tags]
+            for t in range(PACK):
+                at = 0
+                for codes, sc in pieces:
+                    width = codes.shape[1]
+                    nc.tensor.matmul_mx(
+                        out=banks[t // per_bank][:, t % per_bank, at : at + width],
+                        lhsT=w_cols[t],
+                        lhsT_scale=w_sc[:, P * t : P * (t + 1)],
+                        rhs=codes.bitcast(FP8X4),
+                        rhs_scale=sc,
+                        start=True,
+                        stop=True,
+                    )
+                    at = at + width
+            return [(banks[u], slice(u * per_bank, (u + 1) * per_bank)) for u in range(len(tags))]
+
+        wa_cols = [wa_codes[:, 2 * P * t : 2 * P * (t + 1)].bitcast(FP4X4) for t in range(PACK)]
+        x_codes = []
+        wb_cols = []
+
+        def gate_chunk(c, tags):
+            pieces = []
+            for h in range(2):
+                lo, hi = max(cols[c].start, h * HALF) - h * HALF, min(cols[c].stop, (h + 1) * HALF) - h * HALF
+                if lo < hi:
+                    pieces.append((x_codes[h][:, lo:hi], x_sc[h][:, lo:hi]))
+            for bank, ts in product(c, tags, wa_cols, wa_sc, pieces):
+                nc.scalar.activation(gate[c][:, ts, :], bank[:], SILU)
+
+        def up_chunk(c, tags):
+            for bank, ts in product(c, tags, wb_cols, wb_sc, [(z_codes[:, cols[c]], z_sc[:, cols[c]])]):
+                nc.vector.tensor_tensor(prod[c][:, ts, :], bank[:], gate[c][:, ts, :], MULT)
+
+        def add_chunk(c):
+            nc.vector.tensor_tensor(y[c][:], prod[c][:], res_t[c][:], ADD)
+            nc.sync.dma_start(out_rows[:, :, cols[c]], y[c][:])
+            weave(y_bf[c][:], y[c][:])
+
+        def pack_chunk(c):
+            quant(y_codes[:, cols[c]], y_sc[:, cols[c]], y_bf[c][:])
+            nc.sync.dma_start(out_words[:, cols[c]], y_codes[:, cols[c]].bitcast(I32))
+
+        for h in range(2):
+            gather(zg[:, h, :], z_planes[h], z_offs, z_wgt, slice(0, J))
+            x_codes.append(sb([P, HALF], U32, "x_codes%d" % h, tag="z_plane%d" % h))
+            quant(x_codes[h][:], x_sc[h][:], x_bf[h][:])
+            if h == 0:
+                gate_chunk(0, "a")
+                gate_chunk(1, "bc")
+                nc.scalar.copy(
+                    wb_bf[:].rearrange("p (t m i) -> p m i t", t=PACK, i=PACK),
+                    wb_raw[:].rearrange("p i (m t) -> p m i t", t=PACK),
+                )
+        gate_chunk(2, "de")
+        gather(zg[:, 2, :], z_planes[2], z_offs, z_wgt, slice(0, J))
+        wb_codes = sb([P, N], U32, "wb_codes", tag="z_plane2")
+        wb_cols.extend([wb_codes[:, P * t : P * (t + 1)].bitcast(FP8X4) for t in range(PACK)])
+        quant(wb_codes[:], wb_sc[:], wb_bf[:])
+        for c in range(NCH):
+            gather(zg[:, PACK - 1, :], z_planes[PACK - 1], z_offs, z_wgt, cols[c])
+            weave(z_bf[c][:], zg[:, :, cols[c]])
+            quant(z_codes[:, cols[c]], z_sc[:, cols[c]], z_bf[c][:])
+
+        up_chunk(0, "f")
+        gate_chunk(4, "f")
+        up_chunk(1, "gh")
+        gate_chunk(3, "gh")
+        add_chunk(0)
+        add_chunk(1)
+        up_chunk(2, "bc")
+        pack_chunk(0)
+        up_chunk(3, "de")
+        pack_chunk(1)
+        add_chunk(2)
+        up_chunk(4, "a")
+        add_chunk(3)
+        pack_chunk(2)
+        add_chunk(4)
+        pack_chunk(3)
+        pack_chunk(4)
+        for q in range(4):
+            eng = nc.sync if q % 2 == 0 else nc.scalar
+            eng.dma_start(out_scales[4 * q : 4 * q + 4, :], y_sc[32 * q : 32 * q + 4, :].bitcast(I32))

@@ -20,6 +20,7 @@ SILU = mybir.ActivationFunctionType.Silu
 P = 128
 PACK = 4
 HALF = 512
+FIRST = 256
 WIDTHS = [128, 256, 256, 256, 128]
 STARTS = [sum(WIDTHS[:c]) for c in range(len(WIDTHS))]
 NCH = len(WIDTHS)
@@ -47,7 +48,6 @@ def tile_list_glu_resP_kernel(
         wa_codes = sb([P, 2 * N], U8, "wa_codes")
         wa_sc = sb([P, N], U8, "wa_sc")
         wb_raw = sb([P, PACK, N], F32, "wb_raw")
-        wb_bf = sb([P, N * PACK], BF16, "wb_bf")
         wb_sc = sb([P, N], U8, "wb_sc")
         res_t = [sb([P, PACK, WIDTHS[c]], F32, "res%d" % c) for c in range(NCH)]
         warm = sb([P, 2], F32, "warm")
@@ -66,9 +66,9 @@ def tile_list_glu_resP_kernel(
 
         nc.sync.dma_start(x_offs[:], offs)
         nc.sync.dma_start(wa_raw[:].bitcast(I32), wa_words[0].bitcast(I32))
-        nc.sync.dma_start(x_wgt[:, 0:HALF], wgt[:, 0:HALF])
         nc.sync.dma_start(x_planes[0][:], x_rows[:, 0, :])
-        nc.sync.dma_start(x_wgt[:, HALF:J], wgt[:, HALF:J])
+        nc.sync.dma_start(x_wgt[:, 0:FIRST], wgt[:, 0:FIRST])
+        nc.sync.dma_start(x_wgt[:, FIRST:J], wgt[:, FIRST:J])
         for q in range(4):
             nc.sync.dma_start(
                 wa_sc_raw[32 * q : 32 * q + 4, :].bitcast(I32), wa_scales[0, 4 * q : 4 * q + 4, :].bitcast(I32)
@@ -76,8 +76,9 @@ def tile_list_glu_resP_kernel(
         for i in range(1, PACK):
             nc.sync.dma_start(x_planes[i][:], x_rows[:, i, :])
         nc.sync.dma_start(z_offs[:], offs2)
+        nc.sync.dma_start(z_wgt[:, 0:HALF], wgt2[:, 0:HALF])
         nc.sync.dma_start(z_planes[0][:], z_rows[:, 0, :])
-        nc.sync.dma_start(z_wgt[:], wgt2)
+        nc.sync.dma_start(z_wgt[:, HALF:J], wgt2[:, HALF:J])
         nc.sync.dma_start(z_planes[1][:], z_rows[:, 1, :])
         nc.sync.dma_start(wb_raw[:], wb.rearrange("(p i) n -> p i n", i=PACK))
         for i in range(2, PACK):
@@ -106,7 +107,7 @@ def tile_list_glu_resP_kernel(
             )
 
         halves = [slice(0, HALF), slice(HALF, J)]
-        for span in halves:
+        for span in (slice(0, FIRST), slice(FIRST, J)):
             gather(xg[:, 0, :], x_planes[0], x_offs, x_wgt, span)
         nc.vector.tensor_copy(
             wa_sc[:].rearrange("p (t m) -> p m t", t=PACK),
@@ -119,10 +120,12 @@ def tile_list_glu_resP_kernel(
             weave(x_bf[h][:], xg[:, :, halves[h]])
 
         zg = sb([P, PACK, J], F32, "zg")
-        z_bf = [sb([P, WIDTHS[c] * PACK], BF16, "z_bf%d" % c) for c in range(NCH)]
+        wb_bf = zg[:, PACK - 1, :].bitcast(BF16)
+        z_bf = [zg[:, PACK - 1, HALF : HALF + 2 * WIDTHS[0]].bitcast(BF16)]
+        z_bf.extend([sb([P, WIDTHS[c] * PACK], BF16, "z_bf%d" % c)[:] for c in range(1, NCH)])
         z_codes = sb([P, J], U32, "z_codes")
         z_sc = sb([P, J], U8, "z_sc")
-        gate = [sb([P, PACK, WIDTHS[c]], F32, "gate%d" % c) for c in range(NCH)]
+        gate = {}
         prod = [sb([P, PACK, WIDTHS[c]], F32, "prod%d" % c) for c in range(NCH)]
         y = [sb([P, PACK, WIDTHS[c]], F32, "y%d" % c) for c in range(NCH)]
         y_bf = [sb([P, WIDTHS[c] * PACK], BF16, "y_bf%d" % c) for c in range(NCH)]
@@ -161,6 +164,7 @@ def tile_list_glu_resP_kernel(
                 lo, hi = max(cols[c].start, h * HALF) - h * HALF, min(cols[c].stop, (h + 1) * HALF) - h * HALF
                 if lo < hi:
                     pieces.append((x_codes[h][:, lo:hi], x_sc[h][:, lo:hi]))
+            gate[c] = sb([P, PACK, WIDTHS[c]], F32, "gate%d" % c, tag="wb_raw" if c == 2 else None)
             for bank, ts in product(c, tags, wa_cols, wa_sc, pieces):
                 nc.scalar.activation(gate[c][:, ts, :], bank[:], SILU)
 
@@ -178,25 +182,26 @@ def tile_list_glu_resP_kernel(
             nc.sync.dma_start(out_words[:, cols[c]], y_codes[:, cols[c]].bitcast(I32))
 
         for h in range(2):
-            gather(zg[:, h, :], z_planes[h], z_offs, z_wgt, slice(0, J))
+            for span in halves if h == 0 else [slice(0, J)]:
+                gather(zg[:, h, :], z_planes[h], z_offs, z_wgt, span)
             x_codes.append(sb([P, HALF], U32, "x_codes%d" % h, tag="z_plane%d" % h))
             quant(x_codes[h][:], x_sc[h][:], x_bf[h][:])
             if h == 0:
                 gate_chunk(0, "a")
                 gate_chunk(1, "bc")
                 nc.scalar.copy(
-                    wb_bf[:].rearrange("p (t m i) -> p m i t", t=PACK, i=PACK),
+                    wb_bf.rearrange("p (t m i) -> p m i t", t=PACK, i=PACK),
                     wb_raw[:].rearrange("p i (m t) -> p m i t", t=PACK),
                 )
         gate_chunk(2, "de")
         gather(zg[:, 2, :], z_planes[2], z_offs, z_wgt, slice(0, J))
         wb_codes = sb([P, N], U32, "wb_codes", tag="z_plane2")
         wb_cols.extend([wb_codes[:, P * t : P * (t + 1)].bitcast(FP8X4) for t in range(PACK)])
-        quant(wb_codes[:], wb_sc[:], wb_bf[:])
+        quant(wb_codes[:], wb_sc[:], wb_bf)
         for c in range(NCH):
             gather(zg[:, PACK - 1, :], z_planes[PACK - 1], z_offs, z_wgt, cols[c])
-            weave(z_bf[c][:], zg[:, :, cols[c]])
-            quant(z_codes[:, cols[c]], z_sc[:, cols[c]], z_bf[c][:])
+            weave(z_bf[c], zg[:, :, cols[c]])
+            quant(z_codes[:, cols[c]], z_sc[:, cols[c]], z_bf[c])
 
         up_chunk(0, "f")
         gate_chunk(4, "f")

@@ -24,6 +24,7 @@ FIRST = 256
 WIDTHS = [128, 256, 256, 256, 128]
 STARTS = [sum(WIDTHS[:c]) for c in range(len(WIDTHS))]
 NCH = len(WIDTHS)
+SHARED = (1, 2)
 
 
 def tile_list_glu_resP_kernel(
@@ -49,7 +50,9 @@ def tile_list_glu_resP_kernel(
         wa_sc = sb([P, N], U8, "wa_sc")
         wb_raw = sb([P, PACK, N], F32, "wb_raw")
         wb_sc = sb([P, N], U8, "wb_sc")
-        res_t = [sb([P, PACK, WIDTHS[c]], F32, "res%d" % c) for c in range(NCH)]
+        res_y = [sb([P, PACK + (2 if c in SHARED else PACK), WIDTHS[c]], F32, "res_y%d" % c) for c in range(NCH)]
+        res_t = [res_y[c][:, (2 if c in SHARED else PACK) :, :] for c in range(NCH)]
+        y = [res_y[c][:, 0:PACK, :] for c in range(NCH)]
         warm = sb([P, 2], F32, "warm")
 
         cols = [slice(STARTS[c], STARTS[c] + WIDTHS[c]) for c in range(NCH)]
@@ -84,7 +87,7 @@ def tile_list_glu_resP_kernel(
         for i in range(2, PACK):
             nc.sync.dma_start(z_planes[i][:], z_rows[:, i, :])
         for c in range(NCH):
-            nc.sync.dma_start(res_t[c][:], res_rows[:, :, cols[c]])
+            nc.sync.dma_start(res_t[c], res_rows[:, :, cols[c]])
 
         def weave(dst, src):
             nc.scalar.copy(
@@ -127,7 +130,6 @@ def tile_list_glu_resP_kernel(
         z_sc = sb([P, J], U8, "z_sc")
         gate = {}
         prod = [sb([P, PACK, WIDTHS[c]], F32, "prod%d" % c) for c in range(NCH)]
-        y = [sb([P, PACK, WIDTHS[c]], F32, "y%d" % c) for c in range(NCH)]
         y_bf = [sb([P, WIDTHS[c] * PACK], BF16, "y_bf%d" % c) for c in range(NCH)]
         y_codes = sb([P, J], U32, "y_codes")
         y_sc = sb([P, J], U8, "y_sc")
@@ -173,9 +175,19 @@ def tile_list_glu_resP_kernel(
                 nc.vector.tensor_tensor(prod[c][:, ts, :], bank[:], gate[c][:, ts, :], MULT)
 
         def add_chunk(c):
-            nc.vector.tensor_tensor(y[c][:], prod[c][:], res_t[c][:], ADD)
-            nc.sync.dma_start(out_rows[:, :, cols[c]], y[c][:])
-            weave(y_bf[c][:], y[c][:])
+            if c == 0:
+                nc.gpsimd.tensor_tensor(y[c], prod[c][:], res_t[c], ADD)
+            elif c in SHARED:
+                nc.vector.tensor_tensor(y[c][:, 0:2, :], prod[c][:, 0:2, :], res_t[c][:, 0:2, :], ADD)
+                nc.gpsimd.tensor_tensor(y[c][:, 2:4, :], prod[c][:, 2:4, :], res_t[c][:, 2:4, :], ADD)
+            if c < 3:
+                weave(y_bf[c][:], y[c])
+            else:
+                for a in range(0, WIDTHS[c], P):
+                    part = slice(a, a + P)
+                    nc.vector.tensor_tensor(y[c][:, :, part], prod[c][:, :, part], res_t[c][:, :, part], ADD)
+                    weave(y_bf[c][:, PACK * a : PACK * (a + P)], y[c][:, :, part])
+            nc.sync.dma_start(out_rows[:, :, cols[c]], y[c])
 
         def pack_chunk(c):
             quant(y_codes[:, cols[c]], y_sc[:, cols[c]], y_bf[c][:])
@@ -198,26 +210,46 @@ def tile_list_glu_resP_kernel(
         wb_codes = sb([P, N], U32, "wb_codes", tag="z_plane2")
         wb_cols.extend([wb_codes[:, P * t : P * (t + 1)].bitcast(FP8X4) for t in range(PACK)])
         quant(wb_codes[:], wb_sc[:], wb_bf)
-        for c in range(NCH):
+
+        def gather_last(c):
             gather(zg[:, PACK - 1, :], z_planes[PACK - 1], z_offs, z_wgt, cols[c])
+
+        def weave_z(c):
             weave(z_bf[c], zg[:, :, cols[c]])
+
+        def quant_z(c):
             quant(z_codes[:, cols[c]], z_sc[:, cols[c]], z_bf[c])
 
+        gather_last(0)
+        weave_z(0)
+        gather_last(1)
+        weave_z(1)
+        gather_last(4)
+        quant_z(0)
+        gather_last(2)
+        weave_z(2)
+        gather_last(3)
+        weave_z(3)
+        weave_z(4)
+        quant_z(1)
         up_chunk(0, "f")
         gate_chunk(4, "f")
+        add_chunk(0)
+        quant_z(2)
         up_chunk(1, "gh")
         gate_chunk(3, "gh")
-        add_chunk(0)
+        quant_z(3)
         add_chunk(1)
         up_chunk(2, "bc")
+        quant_z(4)
         pack_chunk(0)
+        add_chunk(2)
         up_chunk(3, "de")
         pack_chunk(1)
-        add_chunk(2)
         up_chunk(4, "a")
         add_chunk(3)
-        pack_chunk(2)
         add_chunk(4)
+        pack_chunk(2)
         pack_chunk(3)
         pack_chunk(4)
         for q in range(4):

@@ -19,11 +19,16 @@ SILU = mybir.ActivationFunctionType.Silu
 
 P = 128
 PACK = 4
-HALF = 512
+PAIR = PACK // 2
+GROUP = 16
+QUADS = 4
+LINE = 4
+HALF = J // 2
 FIRST = 256
-WIDTHS = [128, 256, 256, 256, 128]
-STARTS = [sum(WIDTHS[:c]) for c in range(len(WIDTHS))]
-NCH = len(WIDTHS)
+NARROW, WIDE = 128, 256
+WIDTHS = [NARROW, WIDE, WIDE, WIDE, NARROW]
+COLS = [slice(sum(WIDTHS[:c]), sum(WIDTHS[: c + 1])) for c in range(len(WIDTHS))]
+CHUNKS = range(len(WIDTHS))
 SHARED = (1, 2)
 
 
@@ -38,24 +43,24 @@ def tile_list_glu_resP_kernel(
         def sb(shape, dtype, name, tag=None):
             return keep.tile(shape, dtype, name=name, tag=tag or name, align_bytes=64)
 
-        x_offs = keep.tile([P, J // 16], U16, name="x_offs")
-        z_offs = keep.tile([P, J // 16], U16, name="z_offs")
+        x_list = keep.tile([P, J // GROUP], U16, name="x_list")
+        z_list = keep.tile([P, J // GROUP], U16, name="z_list")
         x_planes = [sb([P, T], F32, "x_plane%d" % i) for i in range(PACK)]
         z_planes = [sb([P, T], F32, "z_plane%d" % i) for i in range(PACK)]
         x_wgt = sb([P, J], F32, "x_wgt")
         z_wgt = sb([P, J], F32, "z_wgt")
         wa_raw = sb([P, 2 * N], U8, "wa_raw")
-        wa_sc_raw = sb([P, N], U8, "wa_sc_raw")
+        wa_scales_raw = sb([P, N], U8, "wa_scales_raw")
         wa_codes = sb([P, 2 * N], U8, "wa_codes")
         wa_sc = sb([P, N], U8, "wa_sc")
         wb_raw = sb([P, PACK, N], F32, "wb_raw")
         wb_sc = sb([P, N], U8, "wb_sc")
-        res_y = [sb([P, PACK + (2 if c in SHARED else PACK), WIDTHS[c]], F32, "res_y%d" % c) for c in range(NCH)]
-        res_t = [res_y[c][:, (2 if c in SHARED else PACK) :, :] for c in range(NCH)]
-        y = [res_y[c][:, 0:PACK, :] for c in range(NCH)]
+        res_row = [PAIR if c in SHARED else PACK for c in CHUNKS]
+        res_y = [sb([P, res_row[c] + PACK, WIDTHS[c]], F32, "res_y%d" % c) for c in CHUNKS]
+        res_in = [res_y[c][:, res_row[c] :, :] for c in CHUNKS]
+        y = [res_y[c][:, 0:PACK, :] for c in CHUNKS]
         warm = sb([P, 2], F32, "warm")
 
-        cols = [slice(STARTS[c], STARTS[c] + WIDTHS[c]) for c in range(NCH)]
         x_rows = xT.rearrange("(p i) t -> p i t", i=PACK)
         z_rows = zT.rearrange("(p i) t -> p i t", i=PACK)
         res_rows = res.rearrange("(p t) j -> p t j", t=PACK)
@@ -63,22 +68,23 @@ def tile_list_glu_resP_kernel(
         out_words = out_1[0].rearrange("p j i -> p (j i)").bitcast(I32)
         out_scales = out_2[0].bitcast(I32)
 
-        nc.gpsimd.memset(wa_sc_raw[:].bitcast(I32), 0)
+        nc.gpsimd.memset(wa_scales_raw[:].bitcast(I32), 0)
         nc.gpsimd.memset(warm[:, 0:1], 0.0)
         nc.scalar.activation(warm[:, 1:2], warm[:, 0:1], SILU)
 
-        nc.sync.dma_start(x_offs[:], offs)
+        nc.sync.dma_start(x_list[:], offs)
+        nc.sync.dma_start(z_list[:], offs2)
         nc.sync.dma_start(wa_raw[:].bitcast(I32), wa_words[0].bitcast(I32))
         nc.sync.dma_start(x_planes[0][:], x_rows[:, 0, :])
         nc.sync.dma_start(x_wgt[:, 0:FIRST], wgt[:, 0:FIRST])
         nc.sync.dma_start(x_wgt[:, FIRST:J], wgt[:, FIRST:J])
-        for q in range(4):
-            nc.sync.dma_start(
-                wa_sc_raw[32 * q : 32 * q + 4, :].bitcast(I32), wa_scales[0, 4 * q : 4 * q + 4, :].bitcast(I32)
-            )
-        for i in range(1, PACK):
+        for i in range(1, PACK - 1):
             nc.sync.dma_start(x_planes[i][:], x_rows[:, i, :])
-        nc.sync.dma_start(z_offs[:], offs2)
+        for q in range(QUADS):
+            nc.sync.dma_start(
+                wa_scales_raw[32 * q : 32 * q + 4, :].bitcast(I32), wa_scales[0, 4 * q : 4 * q + 4, :].bitcast(I32)
+            )
+        nc.sync.dma_start(x_planes[PACK - 1][:], x_rows[:, PACK - 1, :])
         nc.sync.dma_start(z_wgt[:, 0:HALF], wgt2[:, 0:HALF])
         nc.sync.dma_start(z_planes[0][:], z_rows[:, 0, :])
         nc.sync.dma_start(z_wgt[:, HALF:J], wgt2[:, HALF:J])
@@ -86,172 +92,202 @@ def tile_list_glu_resP_kernel(
         nc.sync.dma_start(wb_raw[:], wb.rearrange("(p i) n -> p i n", i=PACK))
         for i in range(2, PACK):
             nc.sync.dma_start(z_planes[i][:], z_rows[:, i, :])
-        for c in range(NCH):
-            nc.sync.dma_start(res_t[c], res_rows[:, :, cols[c]])
+        for c in CHUNKS:
+            nc.sync.dma_start(res_in[c], res_rows[:, :, COLS[c]])
 
-        def weave(dst, src):
-            nc.scalar.copy(
-                dst.rearrange("p (c i t) -> p c t i", i=4, t=PACK),
-                src.rearrange("p t (c i) -> p c t i", i=4),
+        def gather(picked, plane, lists, weights, span):
+            entries = lists[:, span.start // GROUP : span.stop // GROUP]
+            nc.vector.tensor_tensor(picked[:, span], plane[:].indirect(entries), weights[:, span], MULT)
+
+        def weave(dst, src, copy=nc.scalar.copy):
+            copy(
+                dst.rearrange("p (c e i) -> p c i e", e=LINE, i=PACK),
+                src.rearrange("p i (c e) -> p c i e", e=LINE),
             )
 
-        nc.vector.tensor_copy(
-            wa_codes[:].rearrange("p (t m b) -> p m t b", t=PACK, b=2),
-            wa_raw[:].rearrange("p (m t b) -> p m t b", t=PACK, b=2),
-        )
-
-        xg = sb([P, PACK, J], F32, "xg")
-        x_bf = [sb([P, HALF * PACK], BF16, "x_bf%d" % h) for h in range(2)]
-        x_sc = [sb([P, HALF], U8, "x_sc%d" % h) for h in range(2)]
-
-        def gather(dst, plane, lists, weights, span):
-            nc.vector.tensor_tensor(
-                dst[:, span], plane[:].indirect(lists[:, span.start // 16 : span.stop // 16]), weights[:, span], MULT
-            )
-
-        halves = [slice(0, HALF), slice(HALF, J)]
-        for span in (slice(0, FIRST), slice(FIRST, J)):
-            gather(xg[:, 0, :], x_planes[0], x_offs, x_wgt, span)
-        nc.vector.tensor_copy(
-            wa_sc[:].rearrange("p (t m) -> p m t", t=PACK),
-            wa_sc_raw[:].rearrange("p (m t) -> p m t", t=PACK),
-        )
-        for i in range(1, PACK - 1):
-            gather(xg[:, i, :], x_planes[i], x_offs, x_wgt, slice(0, J))
-        for h in range(2):
-            gather(xg[:, PACK - 1, :], x_planes[PACK - 1], x_offs, x_wgt, halves[h])
-            weave(x_bf[h][:], xg[:, :, halves[h]])
-
-        zg = sb([P, PACK, J], F32, "zg")
-        wb_bf = zg[:, PACK - 1, :].bitcast(BF16)
-        z_bf = [zg[:, PACK - 1, HALF : HALF + 2 * WIDTHS[0]].bitcast(BF16)]
-        z_bf.extend([sb([P, WIDTHS[c] * PACK], BF16, "z_bf%d" % c)[:] for c in range(1, NCH)])
-        z_codes = sb([P, J], U32, "z_codes")
-        z_sc = sb([P, J], U8, "z_sc")
-        gate = {}
-        prod = [sb([P, PACK, WIDTHS[c]], F32, "prod%d" % c) for c in range(NCH)]
-        y_bf = [sb([P, WIDTHS[c] * PACK], BF16, "y_bf%d" % c) for c in range(NCH)]
-        y_codes = sb([P, J], U32, "y_codes")
-        y_sc = sb([P, J], U8, "y_sc")
-
-        def quant(codes, scales, src):
+        def quantise(codes, scales, src):
             nc.vector.quantize_mx(out=codes.bitcast(FP8X4), scales=scales, in_=src)
 
-        def product(c, tags, w_cols, w_sc, pieces):
-            per_bank = PACK // len(tags)
-            banks = [psum.tile([P, per_bank, WIDTHS[c]], F32, name="ps", tag=tag) for tag in tags]
+        def product(c, bank_tags, w_slices, w_sc, pieces):
+            per_bank = PACK // len(bank_tags)
+            banks = [psum.tile([P, per_bank, WIDTHS[c]], F32, name="bank", tag=tag) for tag in bank_tags]
             for t in range(PACK):
                 at = 0
-                for codes, sc in pieces:
+                for codes, scales in pieces:
                     width = codes.shape[1]
                     nc.tensor.matmul_mx(
                         out=banks[t // per_bank][:, t % per_bank, at : at + width],
-                        lhsT=w_cols[t],
+                        lhsT=w_slices[t],
                         lhsT_scale=w_sc[:, P * t : P * (t + 1)],
                         rhs=codes.bitcast(FP8X4),
-                        rhs_scale=sc,
+                        rhs_scale=scales,
                         start=True,
                         stop=True,
                     )
                     at = at + width
-            return [(banks[u], slice(u * per_bank, (u + 1) * per_bank)) for u in range(len(tags))]
+            return [(banks[u], slice(u * per_bank, (u + 1) * per_bank)) for u in range(len(bank_tags))]
 
-        wa_cols = [wa_codes[:, 2 * P * t : 2 * P * (t + 1)].bitcast(FP4X4) for t in range(PACK)]
-        x_codes = []
-        wb_cols = []
+        nc.vector.tensor_copy(
+            wa_codes[:].rearrange("p (t m b) -> p t m b", t=PACK, b=2),
+            wa_raw[:].rearrange("p (m t b) -> p t m b", t=PACK, b=2),
+        )
+        wa_slices = [wa_codes[:, 2 * P * t : 2 * P * (t + 1)].bitcast(FP4X4) for t in range(PACK)]
 
-        def gate_chunk(c, tags):
+        halves = [slice(0, HALF), slice(HALF, J)]
+        x_picked = sb([P, PACK, J], F32, "x_picked")
+        x_bf = [sb([P, HALF * PACK], BF16, "x_bf%d" % h) for h in range(2)]
+        x_sc = [sb([P, HALF], U8, "x_sc%d" % h) for h in range(2)]
+        for span in (slice(0, FIRST), slice(FIRST, J)):
+            gather(x_picked[:, 0, :], x_planes[0], x_list, x_wgt, span)
+        nc.vector.tensor_copy(
+            wa_sc[:].rearrange("p (t m) -> p t m", t=PACK),
+            wa_scales_raw[:].rearrange("p (m t) -> p t m", t=PACK),
+        )
+        for i in range(1, PACK - 1):
+            gather(x_picked[:, i, :], x_planes[i], x_list, x_wgt, slice(0, J))
+        for h in range(2):
+            gather(x_picked[:, PACK - 1, :], x_planes[PACK - 1], x_list, x_wgt, halves[h])
+            weave(x_bf[h][:], x_picked[:, :, halves[h]])
+
+        z_picked = sb([P, PACK, J], F32, "z_picked")
+        wb_bf = z_picked[:, PACK - 1, :].bitcast(BF16)
+        z_bf = [z_picked[:, PACK - 1, HALF : HALF + 2 * NARROW].bitcast(BF16)]
+        z_bf.extend([sb([P, WIDTHS[c] * PACK], BF16, "z_bf%d" % c)[:] for c in CHUNKS[1:]])
+        z_codes = sb([P, J], U32, "z_codes")
+        z_sc = sb([P, J], U8, "z_sc")
+        y_bf = [sb([P, WIDTHS[c] * PACK], BF16, "y_bf%d" % c) for c in CHUNKS]
+        y_codes = sb([P, J], U32, "y_codes")
+        y_sc = sb([P, J], U8, "y_sc")
+        x_codes = {}
+        gate = {}
+        prod = {}
+
+        def quantise_x(h):
+            x_codes[h] = sb([P, HALF], U32, "x_codes%d" % h, tag="z_plane%d" % h)
+            quantise(x_codes[h][:], x_sc[h][:], x_bf[h][:])
+
+        def gate_product(c, bank_tags):
             pieces = []
             for h in range(2):
-                lo, hi = max(cols[c].start, h * HALF) - h * HALF, min(cols[c].stop, (h + 1) * HALF) - h * HALF
+                lo = max(COLS[c].start, halves[h].start) - halves[h].start
+                hi = min(COLS[c].stop, halves[h].stop) - halves[h].start
                 if lo < hi:
                     pieces.append((x_codes[h][:, lo:hi], x_sc[h][:, lo:hi]))
-            gate[c] = sb([P, PACK, WIDTHS[c]], F32, "gate%d" % c, tag="wb_raw" if c == 2 else None)
-            for bank, ts in product(c, tags, wa_cols, wa_sc, pieces):
-                nc.scalar.activation(gate[c][:, ts, :], bank[:], SILU)
+            return product(c, bank_tags, wa_slices, wa_sc, pieces)
 
-        def up_chunk(c, tags):
-            for bank, ts in product(c, tags, wb_cols, wb_sc, [(z_codes[:, cols[c]], z_sc[:, cols[c]])]):
-                nc.vector.tensor_tensor(prod[c][:, ts, :], bank[:], gate[c][:, ts, :], MULT)
+        def silu(c, banks):
+            for bank, slices in banks:
+                nc.scalar.activation(gate[c][:, slices, :], bank[:], SILU)
 
-        def add_chunk(c):
-            if c == 0:
-                nc.gpsimd.tensor_tensor(y[c], prod[c][:], res_t[c], ADD)
-            elif c in SHARED:
-                nc.vector.tensor_tensor(y[c][:, 0:2, :], prod[c][:, 0:2, :], res_t[c][:, 0:2, :], ADD)
-                nc.gpsimd.tensor_tensor(y[c][:, 2:4, :], prod[c][:, 2:4, :], res_t[c][:, 2:4, :], ADD)
-            if c < 3:
-                weave(y_bf[c][:], y[c])
-            else:
-                for a in range(0, WIDTHS[c], P):
-                    part = slice(a, a + P)
-                    nc.vector.tensor_tensor(y[c][:, :, part], prod[c][:, :, part], res_t[c][:, :, part], ADD)
-                    weave(y_bf[c][:, PACK * a : PACK * (a + P)], y[c][:, :, part])
-            nc.sync.dma_start(out_rows[:, :, cols[c]], y[c])
-
-        def pack_chunk(c):
-            quant(y_codes[:, cols[c]], y_sc[:, cols[c]], y_bf[c][:])
-            nc.sync.dma_start(out_words[:, cols[c]], y_codes[:, cols[c]].bitcast(I32))
-
-        for h in range(2):
-            for span in halves if h == 0 else [slice(0, J)]:
-                gather(zg[:, h, :], z_planes[h], z_offs, z_wgt, span)
-            x_codes.append(sb([P, HALF], U32, "x_codes%d" % h, tag="z_plane%d" % h))
-            quant(x_codes[h][:], x_sc[h][:], x_bf[h][:])
-            if h == 0:
-                gate_chunk(0, "a")
-                gate_chunk(1, "bc")
-                nc.scalar.copy(
-                    wb_bf.rearrange("p (t m i) -> p m i t", t=PACK, i=PACK),
-                    wb_raw[:].rearrange("p i (m t) -> p m i t", t=PACK),
-                )
-        gate_chunk(2, "de")
-        gather(zg[:, 2, :], z_planes[2], z_offs, z_wgt, slice(0, J))
+        for span in halves:
+            gather(z_picked[:, 0, :], z_planes[0], z_list, z_wgt, span)
+        quantise_x(0)
+        for c, bank_tags in ((0, "a"), (1, "bc")):
+            gate[c] = sb([P, PACK, WIDTHS[c]], F32, "gate%d" % c)
+            silu(c, gate_product(c, bank_tags))
+        nc.scalar.copy(
+            wb_bf.rearrange("p (t m i) -> p m i t", t=PACK, i=PACK),
+            wb_raw[:].rearrange("p i (m t) -> p m i t", t=PACK),
+        )
+        gather(z_picked[:, 1, :], z_planes[1], z_list, z_wgt, slice(0, J))
+        quantise_x(1)
+        gate[2] = sb([P, PACK, WIDE], F32, "gate2", tag="wb_raw")
+        silu(2, gate_product(2, "de"))
+        ya_waiting = {3: gate_product(3, "gh"), 4: gate_product(4, "f")}
+        gather(z_picked[:, 2, :], z_planes[2], z_list, z_wgt, slice(0, J))
         wb_codes = sb([P, N], U32, "wb_codes", tag="z_plane2")
-        wb_cols.extend([wb_codes[:, P * t : P * (t + 1)].bitcast(FP8X4) for t in range(PACK)])
-        quant(wb_codes[:], wb_sc[:], wb_bf)
+        wb_slices = [wb_codes[:, P * t : P * (t + 1)].bitcast(FP8X4) for t in range(PACK)]
+        quantise(wb_codes[:], wb_sc[:], wb_bf)
 
         def gather_last(c):
-            gather(zg[:, PACK - 1, :], z_planes[PACK - 1], z_offs, z_wgt, cols[c])
+            gather(z_picked[:, PACK - 1, :], z_planes[PACK - 1], z_list, z_wgt, COLS[c])
 
         def weave_z(c):
-            weave(z_bf[c], zg[:, :, cols[c]])
+            weave(z_bf[c], z_picked[:, :, COLS[c]])
 
-        def quant_z(c):
-            quant(z_codes[:, cols[c]], z_sc[:, cols[c]], z_bf[c])
+        def quantise_z(c):
+            quantise(z_codes[:, COLS[c]], z_sc[:, COLS[c]], z_bf[c])
+
+        def multiply(c, bank_tags, parts):
+            banks = product(c, bank_tags, wb_slices, wb_sc, [(z_codes[:, COLS[c]], z_sc[:, COLS[c]])])
+            for part, (bank, slices) in zip(parts, banks):
+                nc.vector.tensor_tensor(part, bank[:], gate[c][:, slices, :], MULT)
+
+        def multiply_narrow(c, bank_tag):
+            prod[c] = sb([P, PACK, NARROW], F32, "prod%d" % c)
+            multiply(c, bank_tag, [prod[c][:]])
+
+        def multiply_shared(c, bank_tags):
+            prod[c] = [
+                sb([P, PAIR, WIDE], F32, "prod_low%d" % c, tag="prod_low")[:],
+                sb([P, PAIR, WIDE], F32, "prod_high%d" % c)[:],
+            ]
+            multiply(c, bank_tags, prod[c])
+
+        def multiply_wide(c, bank_tags):
+            prod[c] = sb([P, PACK, WIDE], F32, "prod%d" % c, tag="prod_low")
+            multiply(c, bank_tags, [prod[c][:, 0:PAIR, :], prod[c][:, PAIR:PACK, :]])
+
+        def weave_and_store(c):
+            weave(y_bf[c][:], y[c])
+            nc.sync.dma_start(out_rows[:, :, COLS[c]], y[c])
+
+        def add_shared(c):
+            nc.vector.tensor_tensor(y[c][:, 0:PAIR, :], prod[c][0], res_in[c][:, 0:PAIR, :], ADD)
+            nc.gpsimd.tensor_tensor(y[c][:, PAIR:PACK, :], prod[c][1], res_in[c][:, PAIR:PACK, :], ADD)
+            weave_and_store(c)
+
+        def add_and_store(c, first):
+            part = slice(first, first + NARROW)
+            at = COLS[c].start + first
+            nc.vector.tensor_tensor(y[c][:, :, part], prod[c][:, :, part], res_in[c][:, :, part], ADD)
+            nc.sync.dma_start(out_rows[:, :, at : at + NARROW], y[c][:, :, part])
+
+        def pack(c):
+            quantise(y_codes[:, COLS[c]], y_sc[:, COLS[c]], y_bf[c][:])
+            nc.sync.dma_start(out_words[:, COLS[c]], y_codes[:, COLS[c]].bitcast(I32))
 
         gather_last(0)
         weave_z(0)
         gather_last(1)
         weave_z(1)
         gather_last(4)
-        quant_z(0)
+        quantise_z(0)
         gather_last(2)
         weave_z(2)
         gather_last(3)
         weave_z(3)
         weave_z(4)
-        quant_z(1)
-        up_chunk(0, "f")
-        gate_chunk(4, "f")
-        add_chunk(0)
-        quant_z(2)
-        up_chunk(1, "gh")
-        gate_chunk(3, "gh")
-        quant_z(3)
-        add_chunk(1)
-        up_chunk(2, "bc")
-        quant_z(4)
-        pack_chunk(0)
-        add_chunk(2)
-        up_chunk(3, "de")
-        pack_chunk(1)
-        up_chunk(4, "a")
-        add_chunk(3)
-        add_chunk(4)
-        pack_chunk(2)
-        pack_chunk(3)
-        pack_chunk(4)
-        for q in range(4):
-            eng = nc.sync if q % 2 == 0 else nc.scalar
-            eng.dma_start(out_scales[4 * q : 4 * q + 4, :], y_sc[32 * q : 32 * q + 4, :].bitcast(I32))
+        quantise_z(1)
+
+        multiply_narrow(0, "a")
+        nc.gpsimd.tensor_tensor(y[0], prod[0][:], res_in[0], ADD)
+        weave_and_store(0)
+        quantise_z(2)
+        last_gates = sb([P, PACK, WIDE + NARROW], F32, "last_gates", tag="z_picked")
+        gate[3] = last_gates[:, :, 0:WIDE]
+        gate[4] = last_gates[:, :, WIDE:]
+        silu(3, ya_waiting[3])
+        silu(4, ya_waiting[4])
+        multiply_shared(1, "bc")
+        quantise_z(3)
+        add_shared(1)
+        multiply_shared(2, "de")
+        quantise_z(4)
+        pack(0)
+        add_shared(2)
+        multiply_wide(3, "bc")
+        multiply_narrow(4, "a")
+        pack(1)
+
+        for first in range(0, WIDE, NARROW):
+            add_and_store(3, first)
+            weave(y_bf[3][:, PACK * first : PACK * (first + NARROW)], y[3][:, :, first : first + NARROW])
+        add_and_store(4, 0)
+        pack(2)
+        weave(y_bf[4][:], y[4], nc.vector.tensor_copy)
+        pack(3)
+        pack(4)
+        for q in range(QUADS):
+            queue = nc.sync if q % 2 == 0 else nc.scalar
+            queue.dma_start(out_scales[4 * q : 4 * q + 4, :], y_sc[32 * q : 32 * q + 4, :].bitcast(I32))

@@ -59,7 +59,6 @@ def tile_list_glu_resP_kernel(
         res_y = [sb([P, res_row[c] + PACK, WIDTHS[c]], F32, "res_y%d" % c) for c in CHUNKS]
         res_in = [res_y[c][:, res_row[c] :, :] for c in CHUNKS]
         y = [res_y[c][:, 0:PACK, :] for c in CHUNKS]
-        warm = sb([P, 2], F32, "warm")
 
         x_rows = xT.rearrange("(p i) t -> p i t", i=PACK)
         z_rows = zT.rearrange("(p i) t -> p i t", i=PACK)
@@ -69,8 +68,6 @@ def tile_list_glu_resP_kernel(
         out_scales = out_2[0].bitcast(I32)
 
         nc.gpsimd.memset(wa_scales_raw[:].bitcast(I32), 0)
-        nc.gpsimd.memset(warm[:, 0:1], 0.0)
-        nc.scalar.activation(warm[:, 1:2], warm[:, 0:1], SILU)
 
         nc.sync.dma_start(x_list[:], offs)
         nc.sync.dma_start(z_list[:], offs2)
@@ -143,11 +140,21 @@ def tile_list_glu_resP_kernel(
             wa_sc[:].rearrange("p (t m) -> p t m", t=PACK),
             wa_scales_raw[:].rearrange("p (m t) -> p t m", t=PACK),
         )
-        for i in range(1, PACK - 1):
-            gather(x_picked[:, i, :], x_planes[i], x_list, x_wgt, slice(0, J))
+
+        def weave_x_pair(h, first):
+            pair = slice(first, first + 2)
+            nc.scalar.copy(
+                x_bf[h][:].rearrange("p (j i) -> p j i", i=PACK)[:, :, pair],
+                x_picked[:, pair, halves[h]].rearrange("p i j -> p j i"),
+            )
+
+        gather(x_picked[:, 1, :], x_planes[1], x_list, x_wgt, slice(0, J))
         for h in range(2):
-            gather(x_picked[:, PACK - 1, :], x_planes[PACK - 1], x_list, x_wgt, halves[h])
-            weave(x_bf[h][:], x_picked[:, :, halves[h]])
+            weave_x_pair(h, 0)
+        gather(x_picked[:, 2, :], x_planes[2], x_list, x_wgt, slice(0, J))
+        for h in range(2):
+            gather(x_picked[:, 3, :], x_planes[3], x_list, x_wgt, halves[h])
+            weave_x_pair(h, 2)
 
         z_picked = sb([P, PACK, J], F32, "z_picked")
         wb_bf = z_picked[:, PACK - 1, :].bitcast(BF16)
@@ -193,7 +200,9 @@ def tile_list_glu_resP_kernel(
         quantise_x(1)
         gate[2] = sb([P, PACK, WIDE], F32, "gate2", tag="wb_raw")
         silu(2, gate_product(2, "de"))
-        ya_waiting = {3: gate_product(3, "gh"), 4: gate_product(4, "f")}
+        gate[4] = sb([P, PACK, NARROW], F32, "gate4")
+        silu(4, gate_product(4, "f"))
+        ya_waiting = gate_product(3, "gh")
         gather(z_picked[:, 2, :], z_planes[2], z_list, z_wgt, slice(0, J))
         wb_codes = sb([P, N], U32, "wb_codes", tag="z_plane2")
         wb_slices = [wb_codes[:, P * t : P * (t + 1)].bitcast(FP8X4) for t in range(PACK)]
@@ -228,24 +237,29 @@ def tile_list_glu_resP_kernel(
             prod[c] = sb([P, PACK, WIDE], F32, "prod%d" % c, tag="prod_low")
             multiply(c, bank_tags, [prod[c][:, 0:PAIR, :], prod[c][:, PAIR:PACK, :]])
 
-        def weave_and_store(c):
-            weave(y_bf[c][:], y[c])
-            nc.sync.dma_start(out_rows[:, :, COLS[c]], y[c])
+        def store_y(c, slices):
+            nc.sync.dma_start(out_rows[:, slices, COLS[c]], y[c][:, slices, :])
 
         def add_shared(c):
-            nc.vector.tensor_tensor(y[c][:, 0:PAIR, :], prod[c][0], res_in[c][:, 0:PAIR, :], ADD)
-            nc.gpsimd.tensor_tensor(y[c][:, PAIR:PACK, :], prod[c][1], res_in[c][:, PAIR:PACK, :], ADD)
-            weave_and_store(c)
+            for u, engine in enumerate((nc.vector, nc.gpsimd)):
+                slices = slice(PAIR * u, PAIR * (u + 1))
+                engine.tensor_tensor(y[c][:, slices, :], prod[c][u], res_in[c][:, slices, :], ADD)
+                store_y(c, slices)
+            weave(y_bf[c][:], y[c])
 
-        def add_and_store(c, first):
+        def add_narrow(c, first):
             part = slice(first, first + NARROW)
-            at = COLS[c].start + first
             nc.vector.tensor_tensor(y[c][:, :, part], prod[c][:, :, part], res_in[c][:, :, part], ADD)
-            nc.sync.dma_start(out_rows[:, :, at : at + NARROW], y[c][:, :, part])
+
+        def quantise_y(c):
+            quantise(y_codes[:, COLS[c]], y_sc[:, COLS[c]], y_bf[c][:])
+
+        def store_words(span):
+            nc.sync.dma_start(out_words[:, span], y_codes[:, span].bitcast(I32))
 
         def pack(c):
-            quantise(y_codes[:, COLS[c]], y_sc[:, COLS[c]], y_bf[c][:])
-            nc.sync.dma_start(out_words[:, COLS[c]], y_codes[:, COLS[c]].bitcast(I32))
+            quantise_y(c)
+            store_words(COLS[c])
 
         gather_last(0)
         weave_z(0)
@@ -260,15 +274,14 @@ def tile_list_glu_resP_kernel(
         weave_z(4)
         quantise_z(1)
 
+        all_slices = slice(0, PACK)
         multiply_narrow(0, "a")
         nc.gpsimd.tensor_tensor(y[0], prod[0][:], res_in[0], ADD)
-        weave_and_store(0)
+        weave(y_bf[0][:], y[0])
+        store_y(0, all_slices)
         quantise_z(2)
-        last_gates = sb([P, PACK, WIDE + NARROW], F32, "last_gates", tag="z_picked")
-        gate[3] = last_gates[:, :, 0:WIDE]
-        gate[4] = last_gates[:, :, WIDE:]
-        silu(3, ya_waiting[3])
-        silu(4, ya_waiting[4])
+        gate[3] = sb([P, PACK, WIDE], F32, "gate3", tag="z_picked")
+        silu(3, ya_waiting)
         multiply_shared(1, "bc")
         quantise_z(3)
         add_shared(1)
@@ -281,13 +294,16 @@ def tile_list_glu_resP_kernel(
         pack(1)
 
         for first in range(0, WIDE, NARROW):
-            add_and_store(3, first)
+            add_narrow(3, first)
             weave(y_bf[3][:, PACK * first : PACK * (first + NARROW)], y[3][:, :, first : first + NARROW])
-        add_and_store(4, 0)
+        store_y(3, all_slices)
+        add_narrow(4, 0)
+        store_y(4, all_slices)
         pack(2)
         weave(y_bf[4][:], y[4], nc.vector.tensor_copy)
-        pack(3)
-        pack(4)
+        quantise_y(3)
+        quantise_y(4)
+        store_words(slice(COLS[3].start, J))
         for q in range(QUADS):
             queue = nc.sync if q % 2 == 0 else nc.scalar
             queue.dma_start(out_scales[4 * q : 4 * q + 4, :], y_sc[32 * q : 32 * q + 4, :].bitcast(I32))

from contextlib import ExitStack

import concourse.mybir as mybir

K, L, N, T, J = 512, 512, 512, 2048, 1024
FLOPS = 2 * (K + L) * N * J

F32 = mybir.dt.float32
BF16 = mybir.dt.bfloat16
I32 = mybir.dt.int32
U32 = mybir.dt.uint32
U16 = mybir.dt.uint16
U8 = mybir.dt.uint8
FP8X4 = mybir.dt.float8_e4m3fn_x4
FP4X4 = mybir.dt.float4_e2m1fn_x4
MULT = mybir.AluOpType.mult
ADD = mybir.AluOpType.add
SILU = mybir.ActivationFunctionType.Silu

P = 128
PACK = 4
PAIR = PACK // 2
GROUP = 16
QUADS = 4
LINE = 4
HALF = J // 2
FIRST = 256
NARROW, WIDE = 128, 256
WIDTHS = [NARROW, WIDE, WIDE, WIDE, NARROW]
COLS = [slice(sum(WIDTHS[:c]), sum(WIDTHS[: c + 1])) for c in range(len(WIDTHS))]
CHUNKS = range(len(WIDTHS))
SHARED = (1, 2)


def tile_list_glu_resP_kernel(
    tc, xT, wgt, zT, wgt2, wa_words, wa_scales, wb, res, offs, offs2, out_0, out_1, out_2
):
    nc = tc.nc
    with ExitStack() as ctx:
        keep = ctx.enter_context(tc.tile_pool(name="keep", bufs=1))
        psum = ctx.enter_context(tc.psum_pool(name="psum", bufs=1))

        def sb(shape, dtype, name, tag=None):
            return keep.tile(shape, dtype, name=name, tag=tag or name, align_bytes=64)

        x_list = keep.tile([P, J // GROUP], U16, name="x_list")
        z_list = keep.tile([P, J // GROUP], U16, name="z_list")
        x_planes = [sb([P, T], F32, "x_plane%d" % i) for i in range(PACK)]
        z_planes = [sb([P, T], F32, "z_plane%d" % i) for i in range(PACK)]
        x_wgt = sb([P, J], F32, "x_wgt")
        z_wgt = sb([P, J], F32, "z_wgt")
        wa_raw = sb([P, 2 * N], U8, "wa_raw")
        wa_scales_raw = sb([P, N], U8, "wa_scales_raw")
        wa_codes = sb([P, 2 * N], U8, "wa_codes")
        wa_sc = sb([P, N], U8, "wa_sc")
        wb_raw = sb([P, PACK, N], F32, "wb_raw")
        wb_sc = sb([P, N], U8, "wb_sc")
        res_row = [PAIR if c in SHARED else PACK for c in CHUNKS]
        res_y = [sb([P, res_row[c] + PACK, WIDTHS[c]], F32, "res_y%d" % c) for c in CHUNKS]
        res_in = [res_y[c][:, res_row[c] :, :] for c in CHUNKS]
        y = [res_y[c][:, 0:PACK, :] for c in CHUNKS]

        x_rows = xT.rearrange("(p i) t -> p i t", i=PACK)
        z_rows = zT.rearrange("(p i) t -> p i t", i=PACK)
        res_rows = res.rearrange("(p t) j -> p t j", t=PACK)
        out_rows = out_0.rearrange("(p t) j -> p t j", t=PACK)
        out_words = out_1[0].rearrange("p j i -> p (j i)").bitcast(I32)
        out_scales = out_2[0].bitcast(I32)

        nc.gpsimd.memset(wa_scales_raw[:].bitcast(I32), 0)

        nc.sync.dma_start(x_list[:], offs)
        nc.sync.dma_start(z_list[:], offs2)
        nc.sync.dma_start(wa_raw[:].bitcast(I32), wa_words[0].bitcast(I32))
        nc.sync.dma_start(x_planes[0][:], x_rows[:, 0, :])
        nc.sync.dma_start(x_wgt[:, 0:FIRST], wgt[:, 0:FIRST])
        nc.sync.dma_start(x_wgt[:, FIRST:J], wgt[:, FIRST:J])
        for i in range(1, PACK - 1):
            nc.sync.dma_start(x_planes[i][:], x_rows[:, i, :])
        for q in range(QUADS):
            nc.sync.dma_start(
                wa_scales_raw[32 * q : 32 * q + 4, :].bitcast(I32), wa_scales[0, 4 * q : 4 * q + 4, :].bitcast(I32)
            )
        nc.sync.dma_start(x_planes[PACK - 1][:], x_rows[:, PACK - 1, :])
        nc.sync.dma_start(z_wgt[:, 0:HALF], wgt2[:, 0:HALF])
        nc.sync.dma_start(z_planes[0][:], z_rows[:, 0, :])
        nc.sync.dma_start(z_wgt[:, HALF:J], wgt2[:, HALF:J])
        nc.sync.dma_start(z_planes[1][:], z_rows[:, 1, :])
        nc.sync.dma_start(wb_raw[:], wb.rearrange("(p i) n -> p i n", i=PACK))
        for i in range(2, PACK):
            nc.sync.dma_start(z_planes[i][:], z_rows[:, i, :])
        for c in CHUNKS:
            nc.sync.dma_start(res_in[c], res_rows[:, :, COLS[c]])

        def gather(picked, plane, lists, weights, span):
            entries = lists[:, span.start // GROUP : span.stop // GROUP]
            nc.vector.tensor_tensor(picked[:, span], plane[:].indirect(entries), weights[:, span], MULT)

        def weave(dst, src, copy=nc.scalar.copy):
            copy(
                dst.rearrange("p (c e i) -> p c i e", e=LINE, i=PACK),
                src.rearrange("p i (c e) -> p c i e", e=LINE),
            )

        def quantise(codes, scales, src):
            nc.vector.quantize_mx(out=codes.bitcast(FP8X4), scales=scales, in_=src)

        def product(c, bank_tags, w_slices, w_sc, pieces):
            per_bank = PACK // len(bank_tags)
            banks = [psum.tile([P, per_bank, WIDTHS[c]], F32, name="bank", tag=tag) for tag in bank_tags]
            for t in range(PACK):
                at = 0
                for codes, scales in pieces:
                    width = codes.shape[1]
                    nc.tensor.matmul_mx(
                        out=banks[t // per_bank][:, t % per_bank, at : at + width],
                        lhsT=w_slices[t],
                        lhsT_scale=w_sc[:, P * t : P * (t + 1)],
                        rhs=codes.bitcast(FP8X4),
                        rhs_scale=scales,
                        start=True,
                        stop=True,
                    )
                    at = at + width
            return [(banks[u], slice(u * per_bank, (u + 1) * per_bank)) for u in range(len(bank_tags))]

        nc.vector.tensor_copy(
            wa_codes[:].rearrange("p (t m b) -> p t m b", t=PACK, b=2),
            wa_raw[:].rearrange("p (m t b) -> p t m b", t=PACK, b=2),
        )
        wa_slices = [wa_codes[:, 2 * P * t : 2 * P * (t + 1)].bitcast(FP4X4) for t in range(PACK)]

        halves = [slice(0, HALF), slice(HALF, J)]
        x_picked = sb([P, PACK, J], F32, "x_picked")
        x_bf = [sb([P, HALF * PACK], BF16, "x_bf%d" % h) for h in range(2)]
        x_sc = [sb([P, HALF], U8, "x_sc%d" % h) for h in range(2)]
        for span in (slice(0, FIRST), slice(FIRST, J)):
            gather(x_picked[:, 0, :], x_planes[0], x_list, x_wgt, span)
        nc.vector.tensor_copy(
            wa_sc[:].rearrange("p (t m) -> p t m", t=PACK),
            wa_scales_raw[:].rearrange("p (m t) -> p t m", t=PACK),
        )

        def weave_x_pair(h, first):
            pair = slice(first, first + 2)
            nc.scalar.copy(
                x_bf[h][:].rearrange("p (j i) -> p j i", i=PACK)[:, :, pair],
                x_picked[:, pair, halves[h]].rearrange("p i j -> p j i"),
            )

        gather(x_picked[:, 1, :], x_planes[1], x_list, x_wgt, slice(0, J))
        for h in range(2):
            weave_x_pair(h, 0)
        gather(x_picked[:, 2, :], x_planes[2], x_list, x_wgt, slice(0, J))
        for h in range(2):
            gather(x_picked[:, 3, :], x_planes[3], x_list, x_wgt, halves[h])
            weave_x_pair(h, 2)

        z_picked = sb([P, PACK, J], F32, "z_picked")
        wb_bf = z_picked[:, PACK - 1, :].bitcast(BF16)
        z_bf = [z_picked[:, PACK - 1, HALF : HALF + 2 * NARROW].bitcast(BF16)]
        z_bf.extend([sb([P, WIDTHS[c] * PACK], BF16, "z_bf%d" % c)[:] for c in CHUNKS[1:]])
        z_codes = sb([P, J], U32, "z_codes")
        z_sc = sb([P, J], U8, "z_sc")
        y_bf = [sb([P, WIDTHS[c] * PACK], BF16, "y_bf%d" % c) for c in CHUNKS]
        y_codes = sb([P, J], U32, "y_codes")
        y_sc = sb([P, J], U8, "y_sc")
        x_codes = {}
        gate = {}
        prod = {}

        def quantise_x(h):
            x_codes[h] = sb([P, HALF], U32, "x_codes%d" % h, tag="z_plane%d" % h)
            quantise(x_codes[h][:], x_sc[h][:], x_bf[h][:])

        def gate_product(c, bank_tags):
            pieces = []
            for h in range(2):
                lo = max(COLS[c].start, halves[h].start) - halves[h].start
                hi = min(COLS[c].stop, halves[h].stop) - halves[h].start
                if lo < hi:
                    pieces.append((x_codes[h][:, lo:hi], x_sc[h][:, lo:hi]))
            return product(c, bank_tags, wa_slices, wa_sc, pieces)

        def silu(c, banks):
            for bank, slices in banks:
                nc.scalar.activation(gate[c][:, slices, :], bank[:], SILU)

        for span in halves:
            gather(z_picked[:, 0, :], z_planes[0], z_list, z_wgt, span)
        quantise_x(0)
        for c, bank_tags in ((0, "a"), (1, "bc")):
            gate[c] = sb([P, PACK, WIDTHS[c]], F32, "gate%d" % c)
            silu(c, gate_product(c, bank_tags))
        nc.scalar.copy(
            wb_bf.rearrange("p (t m i) -> p m i t", t=PACK, i=PACK),
            wb_raw[:].rearrange("p i (m t) -> p m i t", t=PACK),
        )
        gather(z_picked[:, 1, :], z_planes[1], z_list, z_wgt, slice(0, J))
        quantise_x(1)
        gate[2] = sb([P, PACK, WIDE], F32, "gate2", tag="wb_raw")
        silu(2, gate_product(2, "de"))
        gate[4] = sb([P, PACK, NARROW], F32, "gate4")
        silu(4, gate_product(4, "f"))
        ya_waiting = gate_product(3, "gh")
        gather(z_picked[:, 2, :], z_planes[2], z_list, z_wgt, slice(0, J))
        wb_codes = sb([P, N], U32, "wb_codes", tag="z_plane2")
        wb_slices = [wb_codes[:, P * t : P * (t + 1)].bitcast(FP8X4) for t in range(PACK)]
        quantise(wb_codes[:], wb_sc[:], wb_bf)

        def gather_last(c):
            gather(z_picked[:, PACK - 1, :], z_planes[PACK - 1], z_list, z_wgt, COLS[c])

        def weave_z(c):
            weave(z_bf[c], z_picked[:, :, COLS[c]])

        def quantise_z(c):
            quantise(z_codes[:, COLS[c]], z_sc[:, COLS[c]], z_bf[c])

        def multiply(c, bank_tags, parts):
            banks = product(c, bank_tags, wb_slices, wb_sc, [(z_codes[:, COLS[c]], z_sc[:, COLS[c]])])
            for part, (bank, slices) in zip(parts, banks):
                nc.vector.tensor_tensor(part, bank[:], gate[c][:, slices, :], MULT)

        def multiply_narrow(c, bank_tag):
            prod[c] = sb([P, PACK, NARROW], F32, "prod%d" % c)
            multiply(c, bank_tag, [prod[c][:]])

        def multiply_shared(c, bank_tags):
            prod[c] = [
                sb([P, PAIR, WIDE], F32, "prod_low%d" % c, tag="prod_low")[:],
                sb([P, PAIR, WIDE], F32, "prod_high%d" % c)[:],
            ]
            multiply(c, bank_tags, prod[c])

        def multiply_wide(c, bank_tags):
            prod[c] = sb([P, PACK, WIDE], F32, "prod%d" % c, tag="prod_low")
            multiply(c, bank_tags, [prod[c][:, 0:PAIR, :], prod[c][:, PAIR:PACK, :]])

        def store_y(c, slices):
            nc.sync.dma_start(out_rows[:, slices, COLS[c]], y[c][:, slices, :])

        def add_shared(c):
            for u, engine in enumerate((nc.vector, nc.gpsimd)):
                slices = slice(PAIR * u, PAIR * (u + 1))
                engine.tensor_tensor(y[c][:, slices, :], prod[c][u], res_in[c][:, slices, :], ADD)
                store_y(c, slices)
            weave(y_bf[c][:], y[c])

        def add_narrow(c, first):
            part = slice(first, first + NARROW)
            nc.vector.tensor_tensor(y[c][:, :, part], prod[c][:, :, part], res_in[c][:, :, part], ADD)

        def quantise_y(c):
            quantise(y_codes[:, COLS[c]], y_sc[:, COLS[c]], y_bf[c][:])

        def store_words(span):
            nc.sync.dma_start(out_words[:, span], y_codes[:, span].bitcast(I32))

        def pack(c):
            quantise_y(c)
            store_words(COLS[c])

        gather_last(0)
        weave_z(0)
        gather_last(1)
        weave_z(1)
        gather_last(4)
        quantise_z(0)
        gather_last(2)
        weave_z(2)
        gather_last(3)
        weave_z(3)
        weave_z(4)
        quantise_z(1)

        all_slices = slice(0, PACK)
        multiply_narrow(0, "a")
        nc.gpsimd.tensor_tensor(y[0], prod[0][:], res_in[0], ADD)
        weave(y_bf[0][:], y[0])
        store_y(0, all_slices)
        quantise_z(2)
        gate[3] = sb([P, PACK, WIDE], F32, "gate3", tag="z_picked")
        silu(3, ya_waiting)
        multiply_shared(1, "bc")
        quantise_z(3)
        add_shared(1)
        multiply_shared(2, "de")
        quantise_z(4)
        pack(0)
        add_shared(2)
        multiply_wide(3, "bc")
        multiply_narrow(4, "a")
        pack(1)

        for first in range(0, WIDE, NARROW):
            add_narrow(3, first)
            weave(y_bf[3][:, PACK * first : PACK * (first + NARROW)], y[3][:, :, first : first + NARROW])
        store_y(3, all_slices)
        add_narrow(4, 0)
        store_y(4, all_slices)
        pack(2)
        weave(y_bf[4][:], y[4], nc.vector.tensor_copy)
        quantise_y(3)
        quantise_y(4)
        store_words(slice(COLS[3].start, J))
        for q in range(QUADS):
            queue = nc.sync if q % 2 == 0 else nc.scalar
            queue.dma_start(out_scales[4 * q : 4 * q + 4, :], y_sc[32 * q : 32 * q + 4, :].bitcast(I32))
